import numpy as np
import ml_dtypes


def mxq(x, axis, fmt="e4m3"):
    dtype, down = {"e4m3": (ml_dtypes.float8_e4m3fn, 7), "e5m2": (ml_dtypes.float8_e5m2, 14)}[fmt]
    v = np.moveaxis(np.asarray(x, np.float32).astype(ml_dtypes.bfloat16).astype(np.float64), axis, -1)
    blocks = v.reshape(v.shape[:-1] + (-1, 32))
    amax = np.abs(blocks).max(-1, keepdims=True)
    byte = np.maximum(np.where(amax > 0, np.frexp(amax)[1] - 1 + 127, 0) - down, 1)
    scale = np.exp2(byte - 127.0)
    codes = (blocks / scale).astype(np.float32).astype(dtype).astype(np.float64)
    return np.moveaxis((codes * scale).reshape(v.shape), -1, axis)


WIDE = False


def mx_kscale(k):
    if not WIDE:
        return np.ones(k)
    levels = np.array([10, -10, 5, -5, 0])
    if k % 512:
        return np.exp2(np.random.permutation(np.resize(levels, k // 32))).repeat(32)
    a = np.empty((k // 512, 16))
    for p in range(k // 512):
        a[p, :8] = np.random.permutation(np.resize(levels, 8))
        for g in range(8):
            far = levels[np.abs(levels - a[p, g]) >= 10]
            a[p, g + 8] = far[np.random.randint(len(far))]
    return np.exp2(a.ravel()).repeat(32)


def f64(x):
    return np.asarray(x).astype(np.float64)


def striped(idx):
    return np.tile(idx.reshape(-1, 16).T, (8, 1)).astype(np.uint16)


def unstriped(offs):
    return offs[:16].T.reshape(-1).astype(np.int64)


E2M1 = np.array([0.0, 0.5, 1.0, 1.5, 2.0, 3.0, 4.0, 6.0, -0.0, -0.5, -1.0, -1.5, -2.0, -3.0, -4.0, -6.0])


def pack_weight(w, fmt):
    k, n = w.shape
    w = f64(np.asarray(w, np.float32).astype(ml_dtypes.bfloat16)).reshape(k // 32, 32, n)
    amax = np.abs(w).max(1)
    if fmt == "e4m3":
        byte = np.frexp(amax)[1] - 1 + 127 - 7
    else:
        mant, ex = np.frexp(amax / 6.0)
        byte = np.where(mant > 0.5, ex, ex - 1) + 127
    byte = np.clip(np.where(amax > 0, byte, 1), 1, 254)
    scaled = (w * np.exp2(127.0 - byte)[:, None, :]).reshape(k, n).astype(np.float32)
    by_word = np.ascontiguousarray(scaled.reshape(k // 512, 128, 4, n).transpose(0, 1, 3, 2))
    if fmt == "e4m3":
        words = by_word.astype(ml_dtypes.float8_e4m3fn).view(np.uint8)
    else:
        c = by_word.astype(ml_dtypes.float4_e2m1fn).view(np.uint8) & 0xF
        words = (c[..., 0::2] | (c[..., 1::2] << 4)).reshape(k // 512, 128, 2 * n)
    return np.ascontiguousarray(words), np.ascontiguousarray(byte.astype(np.uint8).reshape(k // 512, 16, n))


def unpack_weight(words, scales, fmt):
    g, _, n = scales.shape
    words = np.ascontiguousarray(words).reshape(g, 128, n, -1)
    if fmt == "e4m3":
        vals = words.view(ml_dtypes.float8_e4m3fn).astype(np.float64)
    else:
        nib = np.empty((g, 128, n, 4), np.uint8)
        nib[..., 0::2] = words & 0xF
        nib[..., 1::2] = words >> 4
        vals = E2M1[nib]
    vals = vals * np.repeat(np.exp2(scales.astype(np.float64) - 127.0), 8, axis=1)[..., None]
    return vals.transpose(0, 1, 3, 2).reshape(g * 512, n)


def gelu(v):
    return 0.5 * v * (1.0 + np.tanh(np.sqrt(2.0 / np.pi) * (v + 0.044715 * v**3)))


K, T, S, S2 = 1024, 2048, 1024, 512


def setup_inputs():
    n = np.random.standard_normal
    s = mx_kscale(K)[:, None]
    d = {}
    d["tab_words"], d["tab_scales"] = pack_weight(n((K, T)) * s, "e4m3")
    d["offs"] = striped(np.random.permutation(T)[:S])
    d["offs2"] = striped(np.random.permutation(T)[:S2])
    d["w1"] = (n((K, K)) / K / s / s.T).astype(np.float32)
    d["w4_words"], d["w4_scales"] = pack_weight(n((K, K)) / K / s / s.T, "e2m1")
    d["gain"] = np.exp(0.4 * n(K)).astype(np.float32)
    d["level"] = (0.7 * n(S2)).astype(np.float32)
    return d


def reference(tab_words, tab_scales, offs, offs2, w1, w4_words, w4_scales, gain, level):
    TW = unpack_weight(tab_words, tab_scales, "e4m3")
    v = TW[:, unstriped(offs)]
    v2 = TW[:, unstriped(offs2)]
    w4 = unpack_weight(w4_words, w4_scales, "e2m1")
    first = mxq(f64(w1), 0, "e4m3").T @ v
    second = w4.T @ v
    h = np.abs(first - f64(gain)[:, None] * second)
    hq = mxq(h, 0, "e4m3")
    e = v2.T @ hq
    z = e - f64(level)[:, None]
    out = z / (1.0 + np.abs(z))
    return out

@@ -1,0 +1,279 @@
+from contextlib import ExitStack
+
+import concourse.mybir as mybir
+
+K, T, S, S2 = 1024, 2048, 1024, 512
+FLOPS = 2 * K * K * S * 2 + 2 * K * S2 * S
+
+F32 = mybir.dt.float32
+BF16 = mybir.dt.bfloat16
+I32 = mybir.dt.int32
+U32 = mybir.dt.uint32
+U16 = mybir.dt.uint16
+U8 = mybir.dt.uint8
+FP8X4 = mybir.dt.float8_e4m3fn_x4
+FP4X4 = mybir.dt.float4_e2m1fn_x4
+ACT = mybir.ActivationFunctionType
+ALU = mybir.AluOpType
+
+P = 128
+PACK = 4
+KP = P * PACK
+PASSES = K // KP
+N = 512
+HALVES = S // N
+QUADS = 4
+MT = S2 // P
+BANKS = 8
+
+
+def tile_list_toolmark_agreement_scores_kernel(
+    tc, tab_words, tab_scales, offs, offs2, w1, w4_words, w4_scales, gain, level, out
+):
+    nc = tc.nc
+    with ExitStack() as ctx:
+        keep = ctx.enter_context(tc.tile_pool(name="keep", bufs=1))
+        stage = ctx.enter_context(tc.tile_pool(name="stage", bufs=1))
+        ring = ctx.enter_context(tc.tile_pool(name="ring", bufs=4))
+        psum = ctx.enter_context(tc.psum_pool(name="psum", bufs=1))
+
+        def kt(shape, dtype, name):
+            return keep.tile(shape, dtype, name=name, align_bytes=64)
+
+        def staged(shape, dtype, slot):
+            return stage.tile(shape, dtype, name="slot%d" % slot, align_bytes=64)
+
+        groups = []
+
+        def next_bank():
+            groups.append(len(groups))
+            return psum.tile([P, N], F32, name="bank%d" % (groups[-1] % BANKS))
+
+        list1 = keep.tile([P, S // 16], U16, name="list1")
+        list2 = keep.tile([P, S2 // 16], U16, name="list2")
+        tab_s = kt([P, T], U8, "tab_s")
+        v_s_up = kt([P, S], U8, "v_s_up")
+        one = kt([P, 1], F32, "one")
+        w4_w_raw = staged([P, PASSES, K], U16, 0)
+        w4_s_raw = staged([P, PASSES, K], U8, 1)
+        nc.vector.memset(tab_s[:].bitcast(I32), 0)
+        nc.gpsimd.memset(w4_s_raw[:].bitcast(I32), 0)
+        nc.vector.memset(v_s_up[:].bitcast(I32), 0)
+        nc.vector.memset(one[:], 1.0)
+
+        nc.sync.dma_start(list1[:], offs)
+        for q in range(QUADS):
+            nc.sync.dma_start(
+                tab_s[32 * q : 32 * q + 8, :].bitcast(I32),
+                tab_scales[:, 4 * q : 4 * q + 4, :].bitcast(I32),
+            )
+        nc.sync.dma_start(list2[:], offs2)
+        gain_t = kt([P, PASSES, PACK], F32, "gain_t")
+        nc.sync.dma_start(gain_t[:], gain.rearrange("(b p i) -> p b i", b=PASSES, i=PACK))
+        for b in range(PASSES):
+            for a in range(PASSES):
+                nc.sync.dma_start(
+                    w4_w_raw[:, a, b * KP : (b + 1) * KP].bitcast(I32),
+                    w4_words[a, :, 2 * b * KP : 2 * (b + 1) * KP].bitcast(I32),
+                )
+        tab_w = kt([P, PASSES * T], U32, "tab_w")
+
+        def load_words(a):
+            nc.sync.dma_start(
+                tab_w[:, a * T : (a + 1) * T].bitcast(I32), tab_words[a].rearrange("p t i -> p (t i)").bitcast(I32)
+            )
+
+        load_words(0)
+        for q in range(QUADS):
+            nc.sync.dma_start(
+                w4_s_raw[32 * q : 32 * q + 4, :, :].bitcast(I32),
+                w4_scales[:, 4 * q : 4 * q + 4, :].rearrange("a r c -> r a c").bitcast(I32),
+            )
+        load_words(1)
+        level_t = kt([P, MT], F32, "level_t")
+        with nc.allow_non_contiguous_dma(reason="one level a partition"):
+            nc.gpsimd.dma_start(level_t[:], level.rearrange("(t p) -> p t", p=P))
+
+        v_s = kt([P, S], U8, "v_s")
+        nc.vector.tensor_copy(v_s[:], tab_s[:].indirect(list1[:]))
+        for q in range(QUADS):
+            nc.scalar.dma_start(
+                v_s_up[32 * q : 32 * q + 4, :].bitcast(I32), v_s[32 * q + 4 : 32 * q + 8, :].bitcast(I32)
+            )
+        v_w = {}
+        cols16 = N // 16
+
+        def gather_words(a, h, stop):
+            v_w[a, h] = kt([P, N], U32, "v_w%d%d" % (a, h))
+            nc.vector.tensor_copy(
+                v_w[a, h][:], tab_w[:, a * T : stop].indirect(list1[:, h * cols16 : (h + 1) * cols16])
+            )
+
+        w4_s = {}
+
+        def deal_w4_scales(b):
+            w4_s[b] = kt([P, PASSES, PACK, P], U8, "w4_s%d" % b)
+            nc.vector.tensor_copy(
+                w4_s[b][:], w4_s_raw[:, :, b * KP : (b + 1) * KP].rearrange("p a (m t) -> p a t m", t=PACK)
+            )
+
+        gather_words(0, 0, T)
+        deal_w4_scales(0)
+        gather_words(1, 0, 2 * T)
+        deal_w4_scales(1)
+        gather_words(0, 1, 2 * T)
+        gather_words(1, 1, 2 * T)
+
+        w4_w = {}
+        for b in range(PASSES):
+            for a in range(PASSES):
+                w4_w[a, b] = kt([P, PACK, P], U16, "w4_w%d%d" % (a, b))
+                nc.scalar.copy(
+                    w4_w[a, b][:], w4_w_raw[:, a, b * KP : (b + 1) * KP].rearrange("p (m t) -> p t m", t=PACK)
+                )
+
+        w1_raw = {}
+        for b in range(PASSES):
+            for a in range(PASSES):
+                w1_raw[a, b] = staged([P, PACK, KP], F32, (2 + a + PASSES * b) % 3)
+                nc.sync.dma_start(
+                    w1_raw[a, b][:],
+                    w1[a * KP : (a + 1) * KP, b * KP : (b + 1) * KP].rearrange("(p j) c -> p j c", j=PACK),
+                )
+
+        order = (1, 0)
+        scaled, diff = {}, {}
+        for b in range(PASSES):
+            for h in range(HALVES):
+                scaled[b, h] = kt([P, PACK, N], F32, "scaled%d%d" % (b, h))
+                diff[b, h] = kt([P, PACK, N], F32, "diff%d%d" % (b, h))
+
+        def second(b, h, slices=range(PACK)):
+            for i in slices:
+                acc = next_bank()
+                for a in order:
+                    nc.tensor.matmul_mx(
+                        acc[:],
+                        lhsT=w4_w[a, b][:, i, :].bitcast(FP4X4),
+                        lhsT_scale=w4_s[b][:, a, i, :],
+                        rhs=v_w[a, h][:].bitcast(FP8X4),
+                        rhs_scale=(v_s, v_s_up)[a][:, h * N : (h + 1) * N],
+                        start=(a == order[0]),
+                        stop=(a == order[-1]),
+                    )
+                nc.scalar.activation(scaled[b, h][:, i, :], acc[:], ACT.Copy, scale=gain_t[:, b, i : i + 1])
+
+        w1_b, w1_w, w1_s = {}, {}, {}
+
+        def round_w1(a, b, copy):
+            w1_b[a, b] = kt([P, PACK * P * PACK], BF16, "w1_b%d%d" % (a, b))
+            copy(
+                w1_b[a, b][:].rearrange("p (t m j) -> p m j t", t=PACK, j=PACK),
+                w1_raw[a, b][:].rearrange("p j (m t) -> p m j t", t=PACK),
+            )
+
+        def quant_w1(a, b):
+            w1_w[a, b] = kt([P, KP], U32, "w1_w%d%d" % (a, b))
+            w1_s[a, b] = kt([P, KP], U8, "w1_s%d%d" % (a, b))
+            nc.vector.quantize_mx(w1_w[a, b][:].bitcast(FP8X4), w1_s[a, b][:], w1_b[a, b][:])
+
+        def first(b, h, slices=range(PACK)):
+            for i in slices:
+                acc = next_bank()
+                ms = slice(i * P, (i + 1) * P)
+                for a in order:
+                    nc.tensor.matmul_mx(
+                        acc[:],
+                        lhsT=w1_w[a, b][:, ms].bitcast(FP8X4),
+                        lhsT_scale=w1_s[a, b][:, ms],
+                        rhs=v_w[a, h][:].bitcast(FP8X4),
+                        rhs_scale=v_s[4 * a : P, h * N : (h + 1) * N],
+                        start=(a == order[0]),
+                        stop=(a == order[-1]),
+                    )
+                nc.vector.tensor_tensor(diff[b, h][:, i, :], acc[:], scaled[b, h][:, i, :], ALU.subtract)
+
+        h_b, h_w, h_s = {}, {}, {}
+
+        def round_h(b, h):
+            h_b[b, h] = kt([P, N * PACK], BF16, "h_b%d%d" % (b, h))
+            nc.scalar.activation(
+                h_b[b, h][:].rearrange("p (c j i) -> p c i j", j=4, i=PACK),
+                diff[b, h][:].rearrange("p i (c j) -> p c i j", j=4),
+                ACT.Abs,
+            )
+
+        def quant_h(b, h):
+            h_w[b, h] = kt([P, N], U32, "h_w%d%d" % (b, h))
+            h_s[b, h] = kt([P, N], U8, "h_s%d%d" % (b, h))
+            nc.vector.quantize_mx(h_w[b, h][:].bitcast(FP8X4), h_s[b, h][:], h_b[b, h][:])
+
+        u = {}
+
+        def gather_u():
+            u["w"] = staged([P, PASSES, S2], U32, 0)
+            u["s"] = staged([P, S2], U8, 1)
+            for a in range(PASSES):
+                nc.vector.tensor_copy(u["w"][:, a, :], tab_w[:, a * T : (a + 1) * T].indirect(list2[:]))
+            nc.vector.tensor_copy(u["s"][:], tab_s[:].indirect(list2[:]))
+
+        def scores(h, tiles=range(MT)):
+            for m in tiles:
+                acc = next_bank()
+                ms = slice(m * P, (m + 1) * P)
+                for b in order:
+                    nc.tensor.matmul_mx(
+                        acc[:],
+                        lhsT=u["w"][:, b, ms].bitcast(FP8X4),
+                        lhsT_scale=u["s"][4 * b : P, ms],
+                        rhs=h_w[b, h][:].bitcast(FP8X4),
+                        rhs_scale=h_s[b, h][:],
+                        start=(b == order[0]),
+                        stop=(b == order[-1]),
+                    )
+                lev = level_t[:, m : m + 1]
+                size = ring.tile([P, N], F32, name="size")
+                nc.scalar.activation(size[:], acc[:], ACT.Abs, bias=lev, scale=-1.0)
+                root = ring.tile([P, N], F32, name="root")
+                nc.scalar.activation(root[:], size[:], ACT.Abs_reciprocal_sqrt, bias=one[:])
+                part = ring.tile([P, N], F32, name="part")
+                nc.vector.scalar_tensor_tensor(part[:], acc[:], lev, root[:], ALU.subtract, ALU.mult)
+                res = ring.tile([P, N], F32, name="res")
+                last = nc.vector if True else nc.gpsimd
+                last.tensor_tensor(res[:], part[:], root[:], ALU.mult)
+                nc.sync.dma_start(out[ms, h * N : (h + 1) * N], res[:])
+
+        on_v, on_s = nc.vector.tensor_copy, nc.scalar.copy
+        second(0, 0)
+        second(1, 0)
+        round_w1(0, 0, on_v)
+        round_w1(1, 0, on_v)
+        quant_w1(0, 0)
+        quant_w1(1, 0)
+        second(0, 1, [0, 1])
+        for i in range(2):
+            first(0, 0, [i])
+            second(0, 1, [i + 2])
+        round_w1(0, 1, on_s)
+        round_w1(1, 1, on_v)
+        quant_w1(0, 1)
+        quant_w1(1, 1)
+        for i in range(2):
+            first(0, 0, [i + 2])
+            second(1, 1, [i])
+        second(1, 1, [2, 3])
+        round_h(0, 0)
+        first(1, 0)
+        gather_u()
+        round_h(1, 0)
+        quant_h(0, 0)
+        first(0, 1)
+        quant_h(1, 0)
+        round_h(0, 1)
+        first(1, 1)
+        scores(0, [0, 1])
+        round_h(1, 1)
+        quant_h(0, 1)
+        scores(0, [2, 3])
+        quant_h(1, 1)
+        scores(1)

@@ -60,6 +60,8 @@ def tile_list_toolmark_agreement_scores_kernel(
         nc.gpsimd.memset(w4_s_raw[:].bitcast(I32), 0)
         nc.vector.memset(v_s_up[:].bitcast(I32), 0)
         nc.vector.memset(one[:], 1.0)
+        warm = kt([P, 1], F32, "warm")
+        nc.scalar.activation(warm[:], one[:], ACT.Abs_reciprocal_sqrt, bias=one[:])
 
         nc.sync.dma_start(list1[:], offs)
         for q in range(QUADS):
@@ -68,20 +70,13 @@ def tile_list_toolmark_agreement_scores_kernel(
                 tab_scales[:, 4 * q : 4 * q + 4, :].bitcast(I32),
             )
         nc.sync.dma_start(list2[:], offs2)
-        gain_t = kt([P, PASSES, PACK], F32, "gain_t")
-        nc.sync.dma_start(gain_t[:], gain.rearrange("(b p i) -> p b i", b=PASSES, i=PACK))
+        gain_t = kt([P, PASSES, 2 * PACK], F32, "gain_t")
         for b in range(PASSES):
-            for a in range(PASSES):
-                nc.sync.dma_start(
-                    w4_w_raw[:, a, b * KP : (b + 1) * KP].bitcast(I32),
-                    w4_words[a, :, 2 * b * KP : 2 * (b + 1) * KP].bitcast(I32),
-                )
-        tab_w = kt([P, PASSES * T], U32, "tab_w")
+            nc.sync.dma_start(gain_t[:, b, 0:PACK], gain[b * KP : (b + 1) * KP].rearrange("(p i) -> p i", i=PACK))
+        tab_w = [kt([P, T], U32, "tab_w%d" % a) for a in range(PASSES)]
 
         def load_words(a):
-            nc.sync.dma_start(
-                tab_w[:, a * T : (a + 1) * T].bitcast(I32), tab_words[a].rearrange("p t i -> p (t i)").bitcast(I32)
-            )
+            nc.sync.dma_start(tab_w[a][:].bitcast(I32), tab_words[a].rearrange("p t i -> p (t i)").bitcast(I32))
 
         load_words(0)
         for q in range(QUADS):
@@ -89,24 +84,30 @@ def tile_list_toolmark_agreement_scores_kernel(
                 w4_s_raw[32 * q : 32 * q + 4, :, :].bitcast(I32),
                 w4_scales[:, 4 * q : 4 * q + 4, :].rearrange("a r c -> r a c").bitcast(I32),
             )
+        nc.sync.dma_start(w4_w_raw[:].bitcast(I32), w4_words.rearrange("a p c -> p a c").bitcast(I32))
         load_words(1)
-        level_t = kt([P, MT], F32, "level_t")
-        with nc.allow_non_contiguous_dma(reason="one level a partition"):
-            nc.gpsimd.dma_start(level_t[:], level.rearrange("(t p) -> p t", p=P))
+
+        w4_w = {}
+        for b in range(PASSES):
+            for a in range(PASSES):
+                w4_w[a, b] = kt([P, PACK, P], U16, "w4_w%d%d" % (a, b))
+                nc.scalar.copy(
+                    w4_w[a, b][:], w4_w_raw[:, a, b * KP : (b + 1) * KP].rearrange("p (m t) -> p t m", t=PACK)
+                )
 
         v_s = kt([P, S], U8, "v_s")
         nc.vector.tensor_copy(v_s[:], tab_s[:].indirect(list1[:]))
         for q in range(QUADS):
-            nc.scalar.dma_start(
+            nc.sync.dma_start(
                 v_s_up[32 * q : 32 * q + 4, :].bitcast(I32), v_s[32 * q + 4 : 32 * q + 8, :].bitcast(I32)
             )
         v_w = {}
         cols16 = N // 16
 
-        def gather_words(a, h, stop):
+        def gather_words(a, h):
             v_w[a, h] = kt([P, N], U32, "v_w%d%d" % (a, h))
             nc.vector.tensor_copy(
-                v_w[a, h][:], tab_w[:, a * T : stop].indirect(list1[:, h * cols16 : (h + 1) * cols16])
+                v_w[a, h][:], tab_w[a][:].indirect(list1[:, h * cols16 : (h + 1) * cols16])
             )
 
         w4_s = {}
@@ -117,25 +118,17 @@ def tile_list_toolmark_agreement_scores_kernel(
                 w4_s[b][:], w4_s_raw[:, :, b * KP : (b + 1) * KP].rearrange("p a (m t) -> p a t m", t=PACK)
             )
 
-        gather_words(0, 0, T)
+        gather_words(0, 0)
+        gather_words(0, 1)
         deal_w4_scales(0)
-        gather_words(1, 0, 2 * T)
+        gather_words(1, 0)
         deal_w4_scales(1)
-        gather_words(0, 1, 2 * T)
-        gather_words(1, 1, 2 * T)
-
-        w4_w = {}
-        for b in range(PASSES):
-            for a in range(PASSES):
-                w4_w[a, b] = kt([P, PACK, P], U16, "w4_w%d%d" % (a, b))
-                nc.scalar.copy(
-                    w4_w[a, b][:], w4_w_raw[:, a, b * KP : (b + 1) * KP].rearrange("p (m t) -> p t m", t=PACK)
-                )
+        gather_words(1, 1)
 
         w1_raw = {}
         for b in range(PASSES):
             for a in range(PASSES):
-                w1_raw[a, b] = staged([P, PACK, KP], F32, (2 + a + PASSES * b) % 3)
+                w1_raw[a, b] = staged([P, PACK, KP], F32, (2 - a - PASSES * b) % 3)
                 nc.sync.dma_start(
                     w1_raw[a, b][:],
                     w1[a * KP : (a + 1) * KP, b * KP : (b + 1) * KP].rearrange("(p j) c -> p j c", j=PACK),
@@ -151,6 +144,7 @@ def tile_list_toolmark_agreement_scores_kernel(
         def second(b, h, slices=range(PACK)):
             for i in slices:
                 acc = next_bank()
+                order = (1, 0) if h else (0, 1)
                 for a in order:
                     nc.tensor.matmul_mx(
                         acc[:],
@@ -211,11 +205,16 @@ def tile_list_toolmark_agreement_scores_kernel(
         u = {}
 
         def gather_u():
-            u["w"] = staged([P, PASSES, S2], U32, 0)
-            u["s"] = staged([P, S2], U8, 1)
+            u["w"] = kt([P, PASSES, S2], U32, "w1_b10")
+            u["s"] = kt([P, S2], U8, "w1_b00")
             for a in range(PASSES):
-                nc.vector.tensor_copy(u["w"][:, a, :], tab_w[:, a * T : (a + 1) * T].indirect(list2[:]))
+                nc.vector.tensor_copy(u["w"][:, a, :], tab_w[a][:].indirect(list2[:]))
             nc.vector.tensor_copy(u["s"][:], tab_s[:].indirect(list2[:]))
+
+        def load_level():
+            u["level"] = kt([P, MT], F32, "w1_b01")
+            with nc.allow_non_contiguous_dma(reason="one level a partition"):
+                nc.sync.dma_start(u["level"][:], level.rearrange("(t p) -> p t", p=P))
 
         def scores(h, tiles=range(MT)):
             for m in tiles:
@@ -231,7 +230,7 @@ def tile_list_toolmark_agreement_scores_kernel(
                         start=(b == order[0]),
                         stop=(b == order[-1]),
                     )
-                lev = level_t[:, m : m + 1]
+                lev = u["level"][:, m : m + 1]
                 size = ring.tile([P, N], F32, name="size")
                 nc.scalar.activation(size[:], acc[:], ACT.Abs, bias=lev, scale=-1.0)
                 root = ring.tile([P, N], F32, name="root")
@@ -251,29 +250,27 @@ def tile_list_toolmark_agreement_scores_kernel(
         quant_w1(0, 0)
         quant_w1(1, 0)
         second(0, 1, [0, 1])
-        for i in range(2):
-            first(0, 0, [i])
-            second(0, 1, [i + 2])
         round_w1(0, 1, on_s)
         round_w1(1, 1, on_v)
         quant_w1(0, 1)
         quant_w1(1, 1)
         for i in range(2):
-            first(0, 0, [i + 2])
-            second(1, 1, [i])
-        second(1, 1, [2, 3])
-        round_h(0, 0)
-        first(1, 0)
+            first(0, 0, [2 * i, 2 * i + 1])
+            second(0, 1, [i + 2])
         gather_u()
+        load_level()
+        round_h(0, 0)
+        for i in range(PACK):
+            first(1, 0, [i])
+            second(1, 1, [i])
         round_h(1, 0)
-        quant_h(0, 0)
         first(0, 1)
+        quant_h(0, 0)
         quant_h(1, 0)
-        round_h(0, 1)
         first(1, 1)
-        scores(0, [0, 1])
+        round_h(0, 1)
         round_h(1, 1)
         quant_h(0, 1)
-        scores(0, [2, 3])
         quant_h(1, 1)
+        scores(0)
         scores(1)

@@ -23,8 +23,13 @@ PASSES = K // KP
 N = 512
 HALVES = S // N
 QUADS = 4
+ROWS = 4
+GROUP = 16
+LINE = 4
 MT = S2 // P
 BANKS = 8
+SLOTS = 3
+DEPTH = 4
 
 
 def tile_list_toolmark_agreement_scores_kernel(
@@ -34,10 +39,10 @@ def tile_list_toolmark_agreement_scores_kernel(
     with ExitStack() as ctx:
         keep = ctx.enter_context(tc.tile_pool(name="keep", bufs=1))
         stage = ctx.enter_context(tc.tile_pool(name="stage", bufs=1))
-        ring = ctx.enter_context(tc.tile_pool(name="ring", bufs=4))
+        ring = ctx.enter_context(tc.tile_pool(name="ring", bufs=DEPTH))
         psum = ctx.enter_context(tc.psum_pool(name="psum", bufs=1))
 
-        def kt(shape, dtype, name):
+        def kept(shape, dtype, name):
             return keep.tile(shape, dtype, name=name, align_bytes=64)
 
         def staged(shape, dtype, slot):
@@ -49,31 +54,31 @@ def tile_list_toolmark_agreement_scores_kernel(
             groups.append(len(groups))
             return psum.tile([P, N], F32, name="bank%d" % (groups[-1] % BANKS))
 
-        list1 = keep.tile([P, S // 16], U16, name="list1")
-        list2 = keep.tile([P, S2 // 16], U16, name="list2")
-        tab_s = kt([P, T], U8, "tab_s")
-        v_s_up = kt([P, S], U8, "v_s_up")
-        one = kt([P, 1], F32, "one")
+        list1 = keep.tile([P, S // GROUP], U16, name="list1")
+        list2 = keep.tile([P, S2 // GROUP], U16, name="list2")
+        tab_s = kept([P, T], U8, "tab_s")
+        v_s_up = kept([P, S], U8, "v_s_up")
+        one = kept([P, 1], F32, "one")
         w4_w_raw = staged([P, PASSES, K], U16, 0)
         w4_s_raw = staged([P, PASSES, K], U8, 1)
         nc.vector.memset(tab_s[:].bitcast(I32), 0)
         nc.gpsimd.memset(w4_s_raw[:].bitcast(I32), 0)
         nc.vector.memset(v_s_up[:].bitcast(I32), 0)
         nc.vector.memset(one[:], 1.0)
-        warm = kt([P, 1], F32, "warm")
+        warm = kept([P, 1], F32, "warm")
         nc.scalar.activation(warm[:], one[:], ACT.Abs_reciprocal_sqrt, bias=one[:])
 
         nc.sync.dma_start(list1[:], offs)
         for q in range(QUADS):
             nc.sync.dma_start(
-                tab_s[32 * q : 32 * q + 8, :].bitcast(I32),
-                tab_scales[:, 4 * q : 4 * q + 4, :].bitcast(I32),
+                tab_s[32 * q : 32 * q + PASSES * ROWS, :].bitcast(I32),
+                tab_scales[:, ROWS * q : ROWS * (q + 1), :].bitcast(I32),
             )
         nc.sync.dma_start(list2[:], offs2)
-        gain_t = kt([P, PASSES, 2 * PACK], F32, "gain_t")
+        gain_t = kept([P, PASSES, 2 * PACK], F32, "gain_t")
         for b in range(PASSES):
             nc.sync.dma_start(gain_t[:, b, 0:PACK], gain[b * KP : (b + 1) * KP].rearrange("(p i) -> p i", i=PACK))
-        tab_w = [kt([P, T], U32, "tab_w%d" % a) for a in range(PASSES)]
+        tab_w = [kept([P, T], U32, "tab_w%d" % a) for a in range(PASSES)]
 
         def load_words(a):
             nc.sync.dma_start(tab_w[a][:].bitcast(I32), tab_words[a].rearrange("p t i -> p (t i)").bitcast(I32))
@@ -81,8 +86,8 @@ def tile_list_toolmark_agreement_scores_kernel(
         load_words(0)
         for q in range(QUADS):
             nc.sync.dma_start(
-                w4_s_raw[32 * q : 32 * q + 4, :, :].bitcast(I32),
-                w4_scales[:, 4 * q : 4 * q + 4, :].rearrange("a r c -> r a c").bitcast(I32),
+                w4_s_raw[32 * q : 32 * q + ROWS, :, :].bitcast(I32),
+                w4_scales[:, ROWS * q : ROWS * (q + 1), :].rearrange("a r c -> r a c").bitcast(I32),
             )
         nc.sync.dma_start(w4_w_raw[:].bitcast(I32), w4_words.rearrange("a p c -> p a c").bitcast(I32))
         load_words(1)
@@ -90,30 +95,31 @@ def tile_list_toolmark_agreement_scores_kernel(
         w4_w = {}
         for b in range(PASSES):
             for a in range(PASSES):
-                w4_w[a, b] = kt([P, PACK, P], U16, "w4_w%d%d" % (a, b))
+                w4_w[a, b] = kept([P, PACK, P], U16, "w4_w%d%d" % (a, b))
                 nc.scalar.copy(
                     w4_w[a, b][:], w4_w_raw[:, a, b * KP : (b + 1) * KP].rearrange("p (m t) -> p t m", t=PACK)
                 )
 
-        v_s = kt([P, S], U8, "v_s")
+        v_s = kept([P, S], U8, "v_s")
         nc.vector.tensor_copy(v_s[:], tab_s[:].indirect(list1[:]))
         for q in range(QUADS):
             nc.sync.dma_start(
-                v_s_up[32 * q : 32 * q + 4, :].bitcast(I32), v_s[32 * q + 4 : 32 * q + 8, :].bitcast(I32)
+                v_s_up[32 * q : 32 * q + ROWS, :].bitcast(I32),
+                v_s[32 * q + ROWS : 32 * q + 2 * ROWS, :].bitcast(I32),
             )
         v_w = {}
-        cols16 = N // 16
+        list_cols = N // GROUP
 
         def gather_words(a, h):
-            v_w[a, h] = kt([P, N], U32, "v_w%d%d" % (a, h))
+            v_w[a, h] = kept([P, N], U32, "v_w%d%d" % (a, h))
             nc.vector.tensor_copy(
-                v_w[a, h][:], tab_w[a][:].indirect(list1[:, h * cols16 : (h + 1) * cols16])
+                v_w[a, h][:], tab_w[a][:].indirect(list1[:, h * list_cols : (h + 1) * list_cols])
             )
 
         w4_s = {}
 
         def deal_w4_scales(b):
-            w4_s[b] = kt([P, PASSES, PACK, P], U8, "w4_s%d" % b)
+            w4_s[b] = kept([P, PASSES, PACK, P], U8, "w4_s%d" % b)
             nc.vector.tensor_copy(
                 w4_s[b][:], w4_s_raw[:, :, b * KP : (b + 1) * KP].rearrange("p a (m t) -> p a t m", t=PACK)
             )
@@ -128,109 +134,109 @@ def tile_list_toolmark_agreement_scores_kernel(
         w1_raw = {}
         for b in range(PASSES):
             for a in range(PASSES):
-                w1_raw[a, b] = staged([P, PACK, KP], F32, (2 - a - PASSES * b) % 3)
+                w1_raw[a, b] = staged([P, PACK, KP], F32, (SLOTS - 1 - a - PASSES * b) % SLOTS)
                 nc.sync.dma_start(
                     w1_raw[a, b][:],
                     w1[a * KP : (a + 1) * KP, b * KP : (b + 1) * KP].rearrange("(p j) c -> p j c", j=PACK),
                 )
 
-        order = (1, 0)
+        late_first = (1, 0)
         scaled, diff = {}, {}
         for b in range(PASSES):
             for h in range(HALVES):
-                scaled[b, h] = kt([P, PACK, N], F32, "scaled%d%d" % (b, h))
-                diff[b, h] = kt([P, PACK, N], F32, "diff%d%d" % (b, h))
+                scaled[b, h] = kept([P, PACK, N], F32, "scaled%d%d" % (b, h))
+                diff[b, h] = kept([P, PACK, N], F32, "diff%d%d" % (b, h))
 
         def second(b, h, slices=range(PACK)):
             for i in slices:
                 acc = next_bank()
-                order = (1, 0) if h else (0, 1)
-                for a in order:
+                passes = late_first if h else (0, 1)
+                for a in passes:
                     nc.tensor.matmul_mx(
                         acc[:],
                         lhsT=w4_w[a, b][:, i, :].bitcast(FP4X4),
                         lhsT_scale=w4_s[b][:, a, i, :],
                         rhs=v_w[a, h][:].bitcast(FP8X4),
                         rhs_scale=(v_s, v_s_up)[a][:, h * N : (h + 1) * N],
-                        start=(a == order[0]),
-                        stop=(a == order[-1]),
+                        start=(a == passes[0]),
+                        stop=(a == passes[-1]),
                     )
                 nc.scalar.activation(scaled[b, h][:, i, :], acc[:], ACT.Copy, scale=gain_t[:, b, i : i + 1])
 
         w1_b, w1_w, w1_s = {}, {}, {}
 
         def round_w1(a, b, copy):
-            w1_b[a, b] = kt([P, PACK * P * PACK], BF16, "w1_b%d%d" % (a, b))
+            w1_b[a, b] = kept([P, PACK * P * PACK], BF16, "w1_b%d%d" % (a, b))
             copy(
                 w1_b[a, b][:].rearrange("p (t m j) -> p m j t", t=PACK, j=PACK),
                 w1_raw[a, b][:].rearrange("p j (m t) -> p m j t", t=PACK),
             )
 
         def quant_w1(a, b):
-            w1_w[a, b] = kt([P, KP], U32, "w1_w%d%d" % (a, b))
-            w1_s[a, b] = kt([P, KP], U8, "w1_s%d%d" % (a, b))
+            w1_w[a, b] = kept([P, KP], U32, "w1_w%d%d" % (a, b))
+            w1_s[a, b] = kept([P, KP], U8, "w1_s%d%d" % (a, b))
             nc.vector.quantize_mx(w1_w[a, b][:].bitcast(FP8X4), w1_s[a, b][:], w1_b[a, b][:])
 
         def first(b, h, slices=range(PACK)):
             for i in slices:
                 acc = next_bank()
                 ms = slice(i * P, (i + 1) * P)
-                for a in order:
+                for a in late_first:
                     nc.tensor.matmul_mx(
                         acc[:],
                         lhsT=w1_w[a, b][:, ms].bitcast(FP8X4),
                         lhsT_scale=w1_s[a, b][:, ms],
                         rhs=v_w[a, h][:].bitcast(FP8X4),
-                        rhs_scale=v_s[4 * a : P, h * N : (h + 1) * N],
-                        start=(a == order[0]),
-                        stop=(a == order[-1]),
+                        rhs_scale=v_s[ROWS * a : P, h * N : (h + 1) * N],
+                        start=(a == late_first[0]),
+                        stop=(a == late_first[-1]),
                     )
                 nc.vector.tensor_tensor(diff[b, h][:, i, :], acc[:], scaled[b, h][:, i, :], ALU.subtract)
 
         h_b, h_w, h_s = {}, {}, {}
 
         def round_h(b, h):
-            h_b[b, h] = kt([P, N * PACK], BF16, "h_b%d%d" % (b, h))
+            h_b[b, h] = kept([P, N * PACK], BF16, "h_b%d%d" % (b, h))
             nc.scalar.activation(
-                h_b[b, h][:].rearrange("p (c j i) -> p c i j", j=4, i=PACK),
-                diff[b, h][:].rearrange("p i (c j) -> p c i j", j=4),
+                h_b[b, h][:].rearrange("p (c j i) -> p c i j", j=LINE, i=PACK),
+                diff[b, h][:].rearrange("p i (c j) -> p c i j", j=LINE),
                 ACT.Abs,
             )
 
         def quant_h(b, h):
-            h_w[b, h] = kt([P, N], U32, "h_w%d%d" % (b, h))
-            h_s[b, h] = kt([P, N], U8, "h_s%d%d" % (b, h))
+            h_w[b, h] = kept([P, N], U32, "h_w%d%d" % (b, h))
+            h_s[b, h] = kept([P, N], U8, "h_s%d%d" % (b, h))
             nc.vector.quantize_mx(h_w[b, h][:].bitcast(FP8X4), h_s[b, h][:], h_b[b, h][:])
 
-        u = {}
+        last_stage = {}
 
-        def gather_u():
-            u["w"] = kt([P, PASSES, S2], U32, "w1_b10")
-            u["s"] = kt([P, S2], U8, "w1_b00")
+        def gather_candidates():
+            last_stage["words"] = kept([P, PASSES, S2], U32, "w1_b10")
+            last_stage["scales"] = kept([P, S2], U8, "w1_b00")
             for a in range(PASSES):
-                nc.vector.tensor_copy(u["w"][:, a, :], tab_w[a][:].indirect(list2[:]))
-            nc.vector.tensor_copy(u["s"][:], tab_s[:].indirect(list2[:]))
+                nc.vector.tensor_copy(last_stage["words"][:, a, :], tab_w[a][:].indirect(list2[:]))
+            nc.vector.tensor_copy(last_stage["scales"][:], tab_s[:].indirect(list2[:]))
 
         def load_level():
-            u["level"] = kt([P, MT], F32, "w1_b01")
+            last_stage["level"] = kept([P, MT], F32, "w1_b01")
             with nc.allow_non_contiguous_dma(reason="one level a partition"):
-                nc.sync.dma_start(u["level"][:], level.rearrange("(t p) -> p t", p=P))
+                nc.sync.dma_start(last_stage["level"][:], level.rearrange("(t p) -> p t", p=P))
 
-        def scores(h, tiles=range(MT)):
-            for m in tiles:
+        def scores(h):
+            for m in range(MT):
                 acc = next_bank()
                 ms = slice(m * P, (m + 1) * P)
-                for b in order:
+                for b in late_first:
                     nc.tensor.matmul_mx(
                         acc[:],
-                        lhsT=u["w"][:, b, ms].bitcast(FP8X4),
-                        lhsT_scale=u["s"][4 * b : P, ms],
+                        lhsT=last_stage["words"][:, b, ms].bitcast(FP8X4),
+                        lhsT_scale=last_stage["scales"][ROWS * b : P, ms],
                         rhs=h_w[b, h][:].bitcast(FP8X4),
                         rhs_scale=h_s[b, h][:],
-                        start=(b == order[0]),
-                        stop=(b == order[-1]),
+                        start=(b == late_first[0]),
+                        stop=(b == late_first[-1]),
                     )
-                lev = u["level"][:, m : m + 1]
+                lev = last_stage["level"][:, m : m + 1]
                 size = ring.tile([P, N], F32, name="size")
                 nc.scalar.activation(size[:], acc[:], ACT.Abs, bias=lev, scale=-1.0)
                 root = ring.tile([P, N], F32, name="root")
@@ -238,39 +244,37 @@ def tile_list_toolmark_agreement_scores_kernel(
                 part = ring.tile([P, N], F32, name="part")
                 nc.vector.scalar_tensor_tensor(part[:], acc[:], lev, root[:], ALU.subtract, ALU.mult)
                 res = ring.tile([P, N], F32, name="res")
-                last = nc.vector if True else nc.gpsimd
-                last.tensor_tensor(res[:], part[:], root[:], ALU.mult)
+                nc.vector.tensor_tensor(res[:], part[:], root[:], ALU.mult)
                 nc.sync.dma_start(out[ms, h * N : (h + 1) * N], res[:])
 
-        on_v, on_s = nc.vector.tensor_copy, nc.scalar.copy
-        second(0, 0)
-        second(1, 0)
-        round_w1(0, 0, on_v)
-        round_w1(1, 0, on_v)
-        quant_w1(0, 0)
-        quant_w1(1, 0)
+        for b in range(PASSES):
+            second(b, 0)
+        for a in range(PASSES):
+            round_w1(a, 0, nc.vector.tensor_copy)
+        for a in range(PASSES):
+            quant_w1(a, 0)
         second(0, 1, [0, 1])
-        round_w1(0, 1, on_s)
-        round_w1(1, 1, on_v)
-        quant_w1(0, 1)
-        quant_w1(1, 1)
         for i in range(2):
             first(0, 0, [2 * i, 2 * i + 1])
             second(0, 1, [i + 2])
-        gather_u()
-        load_level()
-        round_h(0, 0)
         for i in range(PACK):
-            first(1, 0, [i])
             second(1, 1, [i])
-        round_h(1, 0)
-        first(0, 1)
+            first(0, 1, [i])
+        for a in range(PASSES):
+            round_w1(a, 1, nc.scalar.copy)
+        for a in range(PASSES):
+            quant_w1(a, 1)
+        for h in range(HALVES):
+            round_h(0, h)
+        first(1, 0)
+        gather_candidates()
+        load_level()
         quant_h(0, 0)
-        quant_h(1, 0)
+        round_h(1, 0)
         first(1, 1)
-        round_h(0, 1)
-        round_h(1, 1)
         quant_h(0, 1)
+        quant_h(1, 0)
+        round_h(1, 1)
         quant_h(1, 1)
-        scores(0)
-        scores(1)
+        for h in range(HALVES):
+            scores(h)

from contextlib import ExitStack

import concourse.mybir as mybir

K, T, S, S2 = 1024, 2048, 1024, 512
FLOPS = 2 * K * K * S * 2 + 2 * K * S2 * S

F32 = mybir.dt.float32
BF16 = mybir.dt.bfloat16
I32 = mybir.dt.int32
U32 = mybir.dt.uint32
U16 = mybir.dt.uint16
U8 = mybir.dt.uint8
FP8X4 = mybir.dt.float8_e4m3fn_x4
FP4X4 = mybir.dt.float4_e2m1fn_x4
ACT = mybir.ActivationFunctionType
ALU = mybir.AluOpType

P = 128
PACK = 4
KP = P * PACK
PASSES = K // KP
N = 512
HALVES = S // N
QUADS = 4
ROWS = 4
GROUP = 16
LINE = 4
MT = S2 // P
BANKS = 8
SLOTS = 3
DEPTH = 4


def tile_list_toolmark_agreement_scores_kernel(
    tc, tab_words, tab_scales, offs, offs2, w1, w4_words, w4_scales, gain, level, out
):
    nc = tc.nc
    with ExitStack() as ctx:
        keep = ctx.enter_context(tc.tile_pool(name="keep", bufs=1))
        stage = ctx.enter_context(tc.tile_pool(name="stage", bufs=1))
        ring = ctx.enter_context(tc.tile_pool(name="ring", bufs=DEPTH))
        psum = ctx.enter_context(tc.psum_pool(name="psum", bufs=1))

        def kept(shape, dtype, name):
            return keep.tile(shape, dtype, name=name, align_bytes=64)

        def staged(shape, dtype, slot):
            return stage.tile(shape, dtype, name="slot%d" % slot, align_bytes=64)

        groups = []

        def next_bank():
            groups.append(len(groups))
            return psum.tile([P, N], F32, name="bank%d" % (groups[-1] % BANKS))

        list1 = keep.tile([P, S // GROUP], U16, name="list1")
        list2 = keep.tile([P, S2 // GROUP], U16, name="list2")
        tab_s = kept([P, T], U8, "tab_s")
        v_s_up = kept([P, S], U8, "v_s_up")
        one = kept([P, 1], F32, "one")
        w4_w_raw = staged([P, PASSES, K], U16, 0)
        w4_s_raw = staged([P, PASSES, K], U8, 1)
        nc.vector.memset(tab_s[:].bitcast(I32), 0)
        nc.gpsimd.memset(w4_s_raw[:].bitcast(I32), 0)
        nc.vector.memset(v_s_up[:].bitcast(I32), 0)
        nc.vector.memset(one[:], 1.0)
        warm = kept([P, 1], F32, "warm")
        nc.scalar.activation(warm[:], one[:], ACT.Abs_reciprocal_sqrt, bias=one[:])

        nc.sync.dma_start(list1[:], offs)
        for q in range(QUADS):
            nc.sync.dma_start(
                tab_s[32 * q : 32 * q + PASSES * ROWS, :].bitcast(I32),
                tab_scales[:, ROWS * q : ROWS * (q + 1), :].bitcast(I32),
            )
        nc.sync.dma_start(list2[:], offs2)
        gain_t = kept([P, PASSES, 2 * PACK], F32, "gain_t")
        for b in range(PASSES):
            nc.sync.dma_start(gain_t[:, b, 0:PACK], gain[b * KP : (b + 1) * KP].rearrange("(p i) -> p i", i=PACK))
        tab_w = [kept([P, T], U32, "tab_w%d" % a) for a in range(PASSES)]

        def load_words(a):
            nc.sync.dma_start(tab_w[a][:].bitcast(I32), tab_words[a].rearrange("p t i -> p (t i)").bitcast(I32))

        load_words(0)
        for q in range(QUADS):
            nc.sync.dma_start(
                w4_s_raw[32 * q : 32 * q + ROWS, :, :].bitcast(I32),
                w4_scales[:, ROWS * q : ROWS * (q + 1), :].rearrange("a r c -> r a c").bitcast(I32),
            )
        nc.sync.dma_start(w4_w_raw[:].bitcast(I32), w4_words.rearrange("a p c -> p a c").bitcast(I32))
        load_words(1)

        w4_w = {}
        for b in range(PASSES):
            for a in range(PASSES):
                w4_w[a, b] = kept([P, PACK, P], U16, "w4_w%d%d" % (a, b))
                nc.scalar.copy(
                    w4_w[a, b][:], w4_w_raw[:, a, b * KP : (b + 1) * KP].rearrange("p (m t) -> p t m", t=PACK)
                )

        v_s = kept([P, S], U8, "v_s")
        nc.vector.tensor_copy(v_s[:], tab_s[:].indirect(list1[:]))
        for q in range(QUADS):
            nc.sync.dma_start(
                v_s_up[32 * q : 32 * q + ROWS, :].bitcast(I32),
                v_s[32 * q + ROWS : 32 * q + 2 * ROWS, :].bitcast(I32),
            )
        v_w = {}
        list_cols = N // GROUP

        def gather_words(a, h):
            v_w[a, h] = kept([P, N], U32, "v_w%d%d" % (a, h))
            nc.vector.tensor_copy(
                v_w[a, h][:], tab_w[a][:].indirect(list1[:, h * list_cols : (h + 1) * list_cols])
            )

        w4_s = {}

        def deal_w4_scales(b):
            w4_s[b] = kept([P, PASSES, PACK, P], U8, "w4_s%d" % b)
            nc.vector.tensor_copy(
                w4_s[b][:], w4_s_raw[:, :, b * KP : (b + 1) * KP].rearrange("p a (m t) -> p a t m", t=PACK)
            )

        gather_words(0, 0)
        gather_words(0, 1)
        deal_w4_scales(0)
        gather_words(1, 0)
        deal_w4_scales(1)
        gather_words(1, 1)

        w1_raw = {}
        for b in range(PASSES):
            for a in range(PASSES):
                w1_raw[a, b] = staged([P, PACK, KP], F32, (SLOTS - 1 - a - PASSES * b) % SLOTS)
                nc.sync.dma_start(
                    w1_raw[a, b][:],
                    w1[a * KP : (a + 1) * KP, b * KP : (b + 1) * KP].rearrange("(p j) c -> p j c", j=PACK),
                )

        late_first = (1, 0)
        scaled, diff = {}, {}
        for b in range(PASSES):
            for h in range(HALVES):
                scaled[b, h] = kept([P, PACK, N], F32, "scaled%d%d" % (b, h))
                diff[b, h] = kept([P, PACK, N], F32, "diff%d%d" % (b, h))

        def second(b, h, slices=range(PACK)):
            for i in slices:
                acc = next_bank()
                passes = late_first if h else (0, 1)
                for a in passes:
                    nc.tensor.matmul_mx(
                        acc[:],
                        lhsT=w4_w[a, b][:, i, :].bitcast(FP4X4),
                        lhsT_scale=w4_s[b][:, a, i, :],
                        rhs=v_w[a, h][:].bitcast(FP8X4),
                        rhs_scale=(v_s, v_s_up)[a][:, h * N : (h + 1) * N],
                        start=(a == passes[0]),
                        stop=(a == passes[-1]),
                    )
                nc.scalar.activation(scaled[b, h][:, i, :], acc[:], ACT.Copy, scale=gain_t[:, b, i : i + 1])

        w1_b, w1_w, w1_s = {}, {}, {}

        def round_w1(a, b, copy):
            w1_b[a, b] = kept([P, PACK * P * PACK], BF16, "w1_b%d%d" % (a, b))
            copy(
                w1_b[a, b][:].rearrange("p (t m j) -> p m j t", t=PACK, j=PACK),
                w1_raw[a, b][:].rearrange("p j (m t) -> p m j t", t=PACK),
            )

        def quant_w1(a, b):
            w1_w[a, b] = kept([P, KP], U32, "w1_w%d%d" % (a, b))
            w1_s[a, b] = kept([P, KP], U8, "w1_s%d%d" % (a, b))
            nc.vector.quantize_mx(w1_w[a, b][:].bitcast(FP8X4), w1_s[a, b][:], w1_b[a, b][:])

        def first(b, h, slices=range(PACK)):
            for i in slices:
                acc = next_bank()
                ms = slice(i * P, (i + 1) * P)
                for a in late_first:
                    nc.tensor.matmul_mx(
                        acc[:],
                        lhsT=w1_w[a, b][:, ms].bitcast(FP8X4),
                        lhsT_scale=w1_s[a, b][:, ms],
                        rhs=v_w[a, h][:].bitcast(FP8X4),
                        rhs_scale=v_s[ROWS * a : P, h * N : (h + 1) * N],
                        start=(a == late_first[0]),
                        stop=(a == late_first[-1]),
                    )
                nc.vector.tensor_tensor(diff[b, h][:, i, :], acc[:], scaled[b, h][:, i, :], ALU.subtract)

        h_b, h_w, h_s = {}, {}, {}

        def round_h(b, h):
            h_b[b, h] = kept([P, N * PACK], BF16, "h_b%d%d" % (b, h))
            nc.scalar.activation(
                h_b[b, h][:].rearrange("p (c j i) -> p c i j", j=LINE, i=PACK),
                diff[b, h][:].rearrange("p i (c j) -> p c i j", j=LINE),
                ACT.Abs,
            )

        def quant_h(b, h):
            h_w[b, h] = kept([P, N], U32, "h_w%d%d" % (b, h))
            h_s[b, h] = kept([P, N], U8, "h_s%d%d" % (b, h))
            nc.vector.quantize_mx(h_w[b, h][:].bitcast(FP8X4), h_s[b, h][:], h_b[b, h][:])

        last_stage = {}

        def gather_candidates():
            last_stage["words"] = kept([P, PASSES, S2], U32, "w1_b10")
            last_stage["scales"] = kept([P, S2], U8, "w1_b00")
            for a in range(PASSES):
                nc.vector.tensor_copy(last_stage["words"][:, a, :], tab_w[a][:].indirect(list2[:]))
            nc.vector.tensor_copy(last_stage["scales"][:], tab_s[:].indirect(list2[:]))

        def load_level():
            last_stage["level"] = kept([P, MT], F32, "w1_b01")
            with nc.allow_non_contiguous_dma(reason="one level a partition"):
                nc.sync.dma_start(last_stage["level"][:], level.rearrange("(t p) -> p t", p=P))

        def scores(h):
            for m in range(MT):
                acc = next_bank()
                ms = slice(m * P, (m + 1) * P)
                for b in late_first:
                    nc.tensor.matmul_mx(
                        acc[:],
                        lhsT=last_stage["words"][:, b, ms].bitcast(FP8X4),
                        lhsT_scale=last_stage["scales"][ROWS * b : P, ms],
                        rhs=h_w[b, h][:].bitcast(FP8X4),
                        rhs_scale=h_s[b, h][:],
                        start=(b == late_first[0]),
                        stop=(b == late_first[-1]),
                    )
                lev = last_stage["level"][:, m : m + 1]
                size = ring.tile([P, N], F32, name="size")
                nc.scalar.activation(size[:], acc[:], ACT.Abs, bias=lev, scale=-1.0)
                root = ring.tile([P, N], F32, name="root")
                nc.scalar.activation(root[:], size[:], ACT.Abs_reciprocal_sqrt, bias=one[:])
                part = ring.tile([P, N], F32, name="part")
                nc.vector.scalar_tensor_tensor(part[:], acc[:], lev, root[:], ALU.subtract, ALU.mult)
                res = ring.tile([P, N], F32, name="res")
                nc.vector.tensor_tensor(res[:], part[:], root[:], ALU.mult)
                nc.sync.dma_start(out[ms, h * N : (h + 1) * N], res[:])

        for b in range(PASSES):
            second(b, 0)
        for a in range(PASSES):
            round_w1(a, 0, nc.vector.tensor_copy)
        for a in range(PASSES):
            quant_w1(a, 0)
        second(0, 1, [0, 1])
        for i in range(2):
            first(0, 0, [2 * i, 2 * i + 1])
            second(0, 1, [i + 2])
        for i in range(PACK):
            second(1, 1, [i])
            first(0, 1, [i])
        for a in range(PASSES):
            round_w1(a, 1, nc.scalar.copy)
        for a in range(PASSES):
            quant_w1(a, 1)
        for h in range(HALVES):
            round_h(0, h)
        first(1, 0)
        gather_candidates()
        load_level()
        quant_h(0, 0)
        round_h(1, 0)
        first(1, 1)
        quant_h(0, 1)
        quant_h(1, 0)
        round_h(1, 1)
        quant_h(1, 1)
        for h in range(HALVES):
            scores(h)
